import numpy as np, ml_dtypes
CORES = [9,41,49,65,73,81,97,113,15,47,55,71,79,87,103,119]
N = 16
R, NS, T = 256, 512, 128
def entries(a): return a.T.reshape(-1)
def pack(v, P): return np.ascontiguousarray(np.asarray(v, np.int32).reshape(-1, P).T)
def lists(rng, how):
    I = rng.integers(0, N * R, NS)
    if how == "alike": I[:] = rng.integers(N * R)
    if how == "distinct": I = rng.permutation(N * R)[:NS]
    if how == "hotrank": I = R * int(rng.integers(N)) + rng.integers(0, R, NS)
    if how == "edge": I = R * rng.integers(0, N, NS) + np.where(rng.random(NS) < 0.5, 0, R - 1)
    if how == "sorted": I = np.sort(I)
    return {"neg": np.broadcast_to(pack(I, 16), (N, 16, NS // 16)).copy()}
def setup_inputs(rng):
    return dict({"h": rng.standard_normal((N, 128, T), dtype=np.float32).astype(ml_dtypes.bfloat16), "tab": (rng.standard_normal((N, 128, R), dtype=np.float32) / 8).astype(ml_dtypes.bfloat16)}, **lists(rng, "uniform"))
def setup_inputs_alike(rng):
    d = setup_inputs(rng); d.update(lists(rng, "alike"))
    for k in ("h", "tab"): d[k] = (d[k].astype(np.float32) * 1024.0).astype(d[k].dtype)
    return d
def setup_inputs_distinct(rng):
    d = setup_inputs(rng); d.update(lists(rng, "distinct"))
    for k in ("h", "tab"): d[k] = (d[k].astype(np.float32) * (1 / 1024.0)).astype(d[k].dtype)
    return d
def setup_inputs_edge(rng):
    d = setup_inputs(rng); d.update(lists(rng, "edge"))
    return d
def setup_inputs_hotrank(rng):
    d = setup_inputs(rng); d.update(lists(rng, "hotrank"))
    return d
def setup_inputs_sorted(rng):
    d = setup_inputs(rng); d.update(lists(rng, "sorted"))
    return d
def check_inputs(x):
    bad = []
    if x["neg"].min() < 0 or x["neg"].max() >= N * R: bad.append("neg out of range")
    if not all(np.array_equal(a, x["neg"][0]) for a in x["neg"]): bad.append("neg isn't alike on all ranks")
    return bad
def reference(h, tab, neg):
    A = np.concatenate(list(tab), axis=1).astype(np.float64)
    S = A[:, entries(neg[0])]
    return {"y": np.stack([h[r].astype(np.float64).T @ S for r in range(N)]).astype(ml_dtypes.bfloat16)}

@@ -1,0 +1,213 @@
+from concourse.bass import DstId, RemoteDMATransfer
+from concourse.mybir import AluOpType, ActivationFunctionType
+
+N, R, NS, TOK = 16, 256, 512, 128
+WPD = 2
+W = 4
+Q = NS // W
+PAD = 8
+WIN = R + 2 * PAD
+E1 = 16 // W
+
+SCRATCH = {
+    "negs": ("sbuf", [128, NS // 16], "int32"),
+    "offs": ("sbuf", [128, NS // 16], "uint16"),
+    "win": ("sbuf", [128, WIN], "bfloat16"),
+    "hs": ("sbuf", [128, TOK], "bfloat16"),
+    "S": ("sbuf", [128, NS], "bfloat16"),
+    "p0": ("sbuf", [128, Q], "bfloat16"),
+    "p1": ("sbuf", [128, Q], "bfloat16"),
+    "r0": ("sbuf", [128, Q], "bfloat16"),
+    "r1": ("sbuf", [128, Q], "bfloat16"),
+    "r2": ("sbuf", [128, Q], "bfloat16"),
+    "xc": ("sbuf", [128, NS], "bfloat16"),
+    "xr": ("sbuf", [128, NS], "bfloat16"),
+    "xo": ("sbuf", [128, NS], "bfloat16"),
+    "ysb": ("sbuf", [128, NS], "bfloat16"),
+}
+for _q in range(W):
+    SCRATCH["ps%d" % _q] = ("psum", [128, 512], "float32")
+
+SEMAPHORES = ["ldn", "ldt", "ldh", "ms", "so", "gv", "gs", "s1", "s2", "xc", "ls", "cpv", "cps", "st"]
+SEMAPHORES += ["xr%d" % _q for _q in range(W)] + ["xo%d" % _q for _q in range(W)] + ["mm%d" % _q for _q in range(W)]
+
+
+def _bits(mask):
+    return [b for b in range(mask.bit_length()) if (mask >> b) & 1]
+
+
+def _mk(bits):
+    return sum(1 << b for b in bits)
+
+
+def _plan(T, topo):
+    ranks = list(T.cores)
+    ncore = topo.CHIPS * topo.CORES_PER_CHIP
+    chips = sorted(set(topo.chip(c) for c in ranks))
+    sinks = {ch: [c for c in ranks if topo.chip(c) == ch] for ch in chips}
+    workers = {}
+    for ch in chips:
+        able = [k for k in range(ncore) if topo.chip(k) == ch and all(topo.may_write(k, d) for d in ranks if d != k)]
+        able.sort(key=lambda k: (0 if k in ranks else 1, k))
+        pick = []
+        for dd in sorted(set(topo.die(k) for k in able)):
+            pick += [k for k in able if topo.die(k) == dd][:WPD]
+        workers[ch] = pick
+    first = [ch for ch in chips if ch == chips[0] or topo.same_plane(ch, chips[0])]
+    order = first + [ch for ch in chips if ch not in first]
+    half = len(order) // 2
+    groups = [order[:half], order[half:]]
+    partner, free = {}, list(groups[1])
+    for a in groups[0]:
+        m = [b for b in free if topo.mates(a, b)]
+        if m:
+            partner[a] = m[0]
+            free.remove(m[0])
+    for a in groups[0]:
+        if a not in partner:
+            partner[a] = free.pop(0)
+    for a, b in list(partner.items()):
+        partner[b] = a
+    group = {ch: gr for gr in groups for ch in gr}
+    return sinks, workers, group, partner
+
+
+def _dst(topo, c):
+    rid, pid, _se = topo.addr(c)
+    return DstId(rid=rid, pnc=pid)
+
+
+def rank_program(g, core, T, topo):
+    sinks, workers, group, partner = _plan(T, topo)
+    ch = topo.chip(core)
+    if ch not in sinks:
+        return
+    rank = T.rank_of(core)
+    is_worker = core in workers[ch]
+    if rank is None and not is_worker:
+        return
+    sem = T.sem
+    sk = sinks[ch]
+    sent = [0]
+    nv = W // 2
+    myq = workers[ch].index(core) if is_worker else None
+
+    def piece(buf, q):
+        return buf[:, q * Q:(q + 1) * Q]
+
+    if rank is not None:
+        sy, sc, v = g.sync, g.scalar, g.vector
+        sy.dma_start(T.win[:, PAD:PAD + R], T.tab[:, :]).then_inc(sem.ldt, 16)
+        for k in range(8):
+            (sy if k < 3 else sc).dma_start(T.negs[16 * k:16 * k + 16, :], T.neg[:, :]).then_inc(sem.ldn, 16)
+        sy.dma_start(T.hs[:, :], T.h[:, :]).then_inc(sem.ldh, 16)
+        v.memset(T.win[:, 0:PAD], 0.0).then_inc(sem.ms, 1)
+        v.memset(T.win[:, PAD + R:WIN], 0.0).then_inc(sem.ms, 1)
+        v.wait_ge(sem.ldn, 128)
+        v.tensor_scalar(T.offs[:, :], T.negs[:, :], PAD - R * rank, PAD + R, AluOpType.add, AluOpType.min).then_inc(sem.so, 1)
+        oc = NS // 16 // W
+        for eng in (v, sc):
+            eng.wait_ge(sem.so, 1)
+            eng.wait_ge(sem.ms, 2)
+            eng.wait_ge(sem.ldt, 16)
+        for q in range(W):
+            src = T.win[:, 0:WIN].indirect(T.offs[:, q * oc:(q + 1) * oc])
+            if q < nv:
+                v.tensor_copy(piece(T.S, q), src).then_inc(sem.gv, 1)
+            else:
+                sc.activation(piece(T.S, q), src, ActivationFunctionType.Copy).then_inc(sem.gs, 1)
+        g.wait_ge(sem.gv, nv)
+        g.wait_ge(sem.gs, W - nv)
+        slot = "p%d" % sk.index(core)
+        others = [(q, w) for q, w in enumerate(workers[ch]) if w != core]
+        eb = _bits(topo.mask(core, others[0][1]))
+        tr = []
+        for i, (q, w) in enumerate(others):
+            tr.append(RemoteDMATransfer(dst_ids=[_dst(topo, w)], dma_engine_mask=_mk(eb[i * E1:(i + 1) * E1]),
+                                        remote_sem=sem.s1, src=piece(T.S, q), dst=T[slot][:, :]))
+            sent[0] += E1
+        g.remote_dma_fused(tr, local_sem=sem.ls)
+
+    if is_worker:
+        q = myq
+        mine = [piece(T.S, q) if s == core else T["p%d" % i][:, :] for i, s in enumerate(sk)]
+        got = [T.r0[:, :], T.r1[:, :], T.r2[:, :]]
+        peers = [c2 for c2 in group[ch] if c2 != ch]
+        far = sinks[partner[ch]]
+        near = [s for s in sk if s != core]
+        off = topo.mask(core, far[0])
+        for c2 in peers:
+            off &= topo.mask(core, workers[c2][q])
+        for s in far:
+            off &= topo.mask(core, s)
+        on = topo.mask(core, near[0]) & ~off
+        noff, non = len(_bits(off)), len(_bits(on))
+        g.wait_ge(sem.s1, E1 * len(near))
+        dsts = []
+        for c2 in peers:
+            dsts.append(got[[x for x in group[c2] if x != c2].index(ch)])
+        g.remote_dma_fused([RemoteDMATransfer(dst_ids=[_dst(topo, workers[c2][q]) for c2 in peers], dma_engine_mask=off,
+                                              remote_sem=sem.s2, srcs=mine, dsts=dsts, alu_op=1)], local_sem=sem.ls)
+        sent[0] += noff
+        g.remote_dma_fused([RemoteDMATransfer(dst_ids=[_dst(topo, s) for s in near], dma_engine_mask=on,
+                                              remote_sem=sem.xc, srcs=mine, dsts=[piece(T.xc, q) for s in near], alu_op=1)],
+                           local_sem=sem.ls)
+        sent[0] += non
+        g.wait_ge(sem.s2, noff * len(peers))
+        g.remote_dma_fused([
+            RemoteDMATransfer(dst_ids=[_dst(topo, s) for s in far], dma_engine_mask=off, remote_sem=sem["xo%d" % q],
+                              srcs=mine + got, dsts=[piece(T.xo, q) for s in far], alu_op=1),
+            RemoteDMATransfer(dst_ids=[_dst(topo, s) for s in near], dma_engine_mask=on, remote_sem=sem["xr%d" % q],
+                              srcs=got, dsts=[piece(T.xr, q) for s in near], alu_op=1),
+        ], local_sem=sem.ls)
+        sent[0] += noff + non
+
+    if rank is not None:
+        pe = g.tensor
+        some = [w for w in workers[ch] if w != core][0]
+        far_w = workers[partner[ch]][0]
+        n_off = len(_bits(topo.mask(far_w, core)))
+        n_on = len(_bits(topo.mask(some, core) & ~topo.mask(some, sinks[partner[ch]][0])))
+        started = set()
+
+        def mm(qq, rhs, stop=False):
+            ins = pe.matmul(T["ps%d" % qq][:, 0:Q], T.hs[:, :], rhs, qq not in started, stop)
+            started.add(qq)
+            return ins
+
+        pe.wait_ge(sem.ldh, 16)
+        if myq is not None:
+            pe.wait_ge(sem.gv, nv)
+            pe.wait_ge(sem.gs, W - nv)
+            mm(myq, piece(T.S, myq))
+            pe.wait_ge(sem.s1, E1 * (len(sk) - 1))
+            for i, s in enumerate(sk):
+                if s != core:
+                    mm(myq, T["p%d" % i][:, :])
+        rem = [qq for qq in range(W) if qq != myq]
+        pe.wait_ge(sem.xc, n_on * len(rem))
+        for qq in rem:
+            mm(qq, piece(T.xc, qq))
+        if myq is not None:
+            pe.wait_ge(sem.s2, n_off * 3)
+            for b in (T.r0, T.r1, T.r2):
+                mm(myq, b[:, :])
+        for qq in range(W):
+            if qq != myq:
+                pe.wait_ge(sem["xr%d" % qq], n_on)
+                mm(qq, piece(T.xr, qq))
+            pe.wait_ge(sem["xo%d" % qq], n_off)
+            mm(qq, piece(T.xo, qq), True).then_inc(sem["mm%d" % qq], 1)
+        for qq in range(W):
+            if qq < nv:
+                v.wait_ge(sem["mm%d" % qq], 1)
+                v.tensor_copy(piece(T.ysb, qq), T["ps%d" % qq][:, 0:Q]).then_inc(sem.cpv, 1)
+            else:
+                sc.wait_ge(sem["mm%d" % qq], 1)
+                sc.activation(piece(T.ysb, qq), T["ps%d" % qq][:, 0:Q], ActivationFunctionType.Copy).then_inc(sem.cps, 1)
+        sy.wait_ge(sem.cpv, nv)
+        sy.dma_start(T.y[:, 0:nv * Q], T.ysb[:, 0:nv * Q]).then_inc(sem.st, 16)
+        sc.wait_ge(sem.cps, W - nv)
+        sc.dma_start(T.y[:, nv * Q:NS], T.ysb[:, nv * Q:NS]).then_inc(sem.st, 16)
+        g.wait_ge(sem.st, 32)
+    g.wait_ge(sem.ls, sent[0])

@@ -5,6 +5,7 @@ N, R, NS, TOK = 16, 256, 512, 128
 WPD = 2
 W = 4
 Q = NS // W
+GS = 4
 PAD = 8
 WIN = R + 2 * PAD
 E1 = 16 // W
@@ -17,19 +18,27 @@ SCRATCH = {
     "S": ("sbuf", [128, NS], "bfloat16"),
     "p0": ("sbuf", [128, Q], "bfloat16"),
     "p1": ("sbuf", [128, Q], "bfloat16"),
-    "r0": ("sbuf", [128, Q], "bfloat16"),
-    "r1": ("sbuf", [128, Q], "bfloat16"),
-    "r2": ("sbuf", [128, Q], "bfloat16"),
+    "am": ("sbuf", [128, Q], "bfloat16"),
+    "b0": ("sbuf", [128, Q], "bfloat16"),
+    "b1": ("sbuf", [128, Q], "bfloat16"),
+    "xrs": ("sbuf", [128, Q], "bfloat16"),
+    "ones": ("sbuf", [128, 128], "bfloat16"),
+    "ident": ("sbuf", [128, 128], "bfloat16"),
     "xc": ("sbuf", [128, NS], "bfloat16"),
     "xr": ("sbuf", [128, NS], "bfloat16"),
     "xo": ("sbuf", [128, NS], "bfloat16"),
     "ysb": ("sbuf", [128, NS], "bfloat16"),
+    "psr": ("psum", [128, 512], "float32"),
 }
 for _q in range(W):
     SCRATCH["ps%d" % _q] = ("psum", [128, 512], "float32")
+for _q in range(GS):
+    SCRATCH["r%d" % _q] = ("sbuf", [128, Q], "bfloat16")
 
-SEMAPHORES = ["ldn", "ldt", "ldh", "ms", "so", "gv", "gs", "s1", "s2", "xc", "ls", "cpv", "cps", "st"]
+SEMAPHORES = ["ldn", "ldt", "ldh", "ms", "so", "gv", "gs", "gv2", "gs2", "s1", "xc", "ls", "cpv", "cps", "st",
+              "va", "vx", "mi", "idn", "pr", "sr"]
 SEMAPHORES += ["xr%d" % _q for _q in range(W)] + ["xo%d" % _q for _q in range(W)] + ["mm%d" % _q for _q in range(W)]
+SEMAPHORES += ["s2%d" % _q for _q in range(GS)]
 
 
 def _bits(mask):
@@ -52,11 +61,11 @@ def _plan(T, topo):
         pick = []
         for dd in sorted(set(topo.die(k) for k in able)):
             pick += [k for k in able if topo.die(k) == dd][:WPD]
+        pick.sort(key=lambda k: (0 if k in ranks else 1, topo.die(k), k))
         workers[ch] = pick
     first = [ch for ch in chips if ch == chips[0] or topo.same_plane(ch, chips[0])]
     order = first + [ch for ch in chips if ch not in first]
-    half = len(order) // 2
-    groups = [order[:half], order[half:]]
+    groups = [order[:GS], order[GS:]]
     partner, free = {}, list(groups[1])
     for a in groups[0]:
         m = [b for b in free if topo.mates(a, b)]
@@ -91,79 +100,119 @@ def rank_program(g, core, T, topo):
     sent = [0]
     nv = W // 2
     myq = workers[ch].index(core) if is_worker else None
+    sy, sc, v, pe = g.sync, g.scalar, g.vector, g.tensor
+    ADD = AluOpType.add
+    COPY = ActivationFunctionType.Copy
 
     def piece(buf, q):
         return buf[:, q * Q:(q + 1) * Q]
 
     if rank is not None:
-        sy, sc, v = g.sync, g.scalar, g.vector
         sy.dma_start(T.win[:, PAD:PAD + R], T.tab[:, :]).then_inc(sem.ldt, 16)
         for k in range(8):
             (sy if k < 3 else sc).dma_start(T.negs[16 * k:16 * k + 16, :], T.neg[:, :]).then_inc(sem.ldn, 16)
         sy.dma_start(T.hs[:, :], T.h[:, :]).then_inc(sem.ldh, 16)
         v.memset(T.win[:, 0:PAD], 0.0).then_inc(sem.ms, 1)
         v.memset(T.win[:, PAD + R:WIN], 0.0).then_inc(sem.ms, 1)
+    if is_worker:
+        v.memset(T.ones[:, :], 1.0).then_inc(sem.mi, 1)
+        g.wait_ge(sem.mi, 1)
+        g.affine_select(T.ident[:, :], T.ones[:, :], [[-1, 128]], AluOpType.is_equal, 0.0, 0, 1).then_inc(sem.idn, 1)
+    if rank is not None:
         v.wait_ge(sem.ldn, 128)
-        v.tensor_scalar(T.offs[:, :], T.negs[:, :], PAD - R * rank, PAD + R, AluOpType.add, AluOpType.min).then_inc(sem.so, 1)
-        oc = NS // 16 // W
+        v.tensor_scalar(T.offs[:, :], T.negs[:, :], PAD - R * rank, PAD + R, ADD, AluOpType.min).then_inc(sem.so, 1)
         for eng in (v, sc):
             eng.wait_ge(sem.so, 1)
             eng.wait_ge(sem.ms, 2)
             eng.wait_ge(sem.ldt, 16)
-        for q in range(W):
-            src = T.win[:, 0:WIN].indirect(T.offs[:, q * oc:(q + 1) * oc])
-            if q < nv:
-                v.tensor_copy(piece(T.S, q), src).then_inc(sem.gv, 1)
-            else:
-                sc.activation(piece(T.S, q), src, ActivationFunctionType.Copy).then_inc(sem.gs, 1)
-        g.wait_ge(sem.gv, nv)
-        g.wait_ge(sem.gs, W - nv)
+
+        def gath(a, b):
+            return T.S[:, a:b], T.win[:, 0:WIN].indirect(T.offs[:, a // 16:b // 16])
+
+        late = Q * len([w for w in workers[ch] if w in sk])
+        mid = late + (NS - late) // 2
+        o, i_ = gath(late, mid)
+        v.tensor_copy(o, i_).then_inc(sem.gv, 1)
+        o, i_ = gath(mid, NS)
+        sc.activation(o, i_, COPY).then_inc(sem.gs, 1)
+        o, i_ = gath(0, late // 2)
+        v.tensor_copy(o, i_).then_inc(sem.gv2, 1)
+        o, i_ = gath(late // 2, late)
+        sc.activation(o, i_, COPY).then_inc(sem.gs2, 1)
         slot = "p%d" % sk.index(core)
         others = [(q, w) for q, w in enumerate(workers[ch]) if w != core]
         eb = _bits(topo.mask(core, others[0][1]))
-        tr = []
-        for i, (q, w) in enumerate(others):
-            tr.append(RemoteDMATransfer(dst_ids=[_dst(topo, w)], dma_engine_mask=_mk(eb[i * E1:(i + 1) * E1]),
-                                        remote_sem=sem.s1, src=piece(T.S, q), dst=T[slot][:, :]))
-            sent[0] += E1
-        g.remote_dma_fused(tr, local_sem=sem.ls)
+        calls = [[(q, w) for q, w in others if w not in sk], [(q, w) for q, w in others if w in sk]]
+        used = 0
+        for n, lst in enumerate(calls):
+            g.wait_ge(sem.gv2 if n else sem.gv, 1)
+            g.wait_ge(sem.gs2 if n else sem.gs, 1)
+            tr = []
+            for q, w in lst:
+                tr.append(RemoteDMATransfer(dst_ids=[_dst(topo, w)], dma_engine_mask=_mk(eb[used:used + E1]),
+                                            remote_sem=sem.s1, src=piece(T.S, q), dst=T[slot][:, :]))
+                used += E1
+                sent[0] += E1
+            if tr:
+                g.remote_dma_fused(tr, local_sem=sem.ls)
 
     if is_worker:
         q = myq
         mine = [piece(T.S, q) if s == core else T["p%d" % i][:, :] for i, s in enumerate(sk)]
-        got = [T.r0[:, :], T.r1[:, :], T.r2[:, :]]
-        peers = [c2 for c2 in group[ch] if c2 != ch]
+        gr = group[ch]
+        gi = gr.index(ch)
+        to = [gr[(gi + k) % GS] for k in range(1, GS)]
+        frm = [(gi - k) % GS for k in range(1, GS)]
+        last = T["r%d" % frm[-1]]
         far = sinks[partner[ch]]
         near = [s for s in sk if s != core]
         off = topo.mask(core, far[0])
-        for c2 in peers:
+        for c2 in to:
             off &= topo.mask(core, workers[c2][q])
         for s in far:
             off &= topo.mask(core, s)
         on = topo.mask(core, near[0]) & ~off
         noff, non = len(_bits(off)), len(_bits(on))
         g.wait_ge(sem.s1, E1 * len(near))
-        dsts = []
-        for c2 in peers:
-            dsts.append(got[[x for x in group[c2] if x != c2].index(ch)])
-        g.remote_dma_fused([RemoteDMATransfer(dst_ids=[_dst(topo, workers[c2][q]) for c2 in peers], dma_engine_mask=off,
-                                              remote_sem=sem.s2, srcs=mine, dsts=dsts, alu_op=1)], local_sem=sem.ls)
+        g.remote_dma_fused([RemoteDMATransfer(dst_ids=[_dst(topo, workers[c2][q]) for c2 in to], dma_engine_mask=off,
+                                              remote_sem=sem["s2%d" % gi], srcs=mine,
+                                              dsts=[T["r%d" % gi][:, :] for c2 in to], alu_op=1)], local_sem=sem.ls)
         sent[0] += noff
         g.remote_dma_fused([RemoteDMATransfer(dst_ids=[_dst(topo, s) for s in near], dma_engine_mask=on,
-                                              remote_sem=sem.xc, srcs=mine, dsts=[piece(T.xc, q) for s in near], alu_op=1)],
-                           local_sem=sem.ls)
+                                              remote_sem=sem.xc, srcs=mine,
+                                              dsts=[piece(T.xc, q) for s in near], alu_op=1)], local_sem=sem.ls)
         sent[0] += non
-        g.wait_ge(sem.s2, noff * len(peers))
+        v.wait_ge(sem.s1, E1 * len(near))
+        if rank is not None:
+            v.wait_ge(sem.gv2, 1)
+            v.wait_ge(sem.gs2, 1)
+        v.tensor_tensor(T.am[:, :], mine[0], mine[1], ADD).then_inc(sem.va, 1)
+        v.wait_ge(sem.va, 1)
+        pe.wait_ge(sem.idn, 1)
+        prev = T.am
+        for k, s in enumerate(frm[:-1]):
+            arr = T["r%d" % s]
+            v.wait_ge(sem["s2%d" % s], noff)
+            v.wait_ge(sem.vx, k)
+            v.tensor_tensor(T["b%d" % k][:, :], prev[:, :], arr[:, :], ADD).then_inc(sem.vx, 1)
+            prev = T["b%d" % k]
+            pe.wait_ge(sem["s2%d" % s], noff)
+            ins = pe.matmul(T.psr[:, 0:Q], T.ident[:, :], arr[:, :], k == 0, k == GS - 3)
+        ins.then_inc(sem.pr, 1)
+        sc.wait_ge(sem.pr, 1)
+        sc.activation(T.xrs[:, :], T.psr[:, 0:Q], COPY).then_inc(sem.sr, 1)
+        g.wait_ge(sem.vx, GS - 2)
+        g.wait_ge(sem.sr, 1)
+        g.wait_ge(sem["s2%d" % frm[-1]], noff)
         g.remote_dma_fused([
             RemoteDMATransfer(dst_ids=[_dst(topo, s) for s in far], dma_engine_mask=off, remote_sem=sem["xo%d" % q],
-                              srcs=mine + got, dsts=[piece(T.xo, q) for s in far], alu_op=1),
+                              srcs=[prev[:, :], last[:, :]], dsts=[piece(T.xo, q) for s in far], alu_op=1),
             RemoteDMATransfer(dst_ids=[_dst(topo, s) for s in near], dma_engine_mask=on, remote_sem=sem["xr%d" % q],
-                              srcs=got, dsts=[piece(T.xr, q) for s in near], alu_op=1),
+                              srcs=[T.xrs[:, :], last[:, :]], dsts=[piece(T.xr, q) for s in near], alu_op=1),
         ], local_sem=sem.ls)
         sent[0] += noff + non
 
     if rank is not None:
-        pe = g.tensor
         some = [w for w in workers[ch] if w != core][0]
         far_w = workers[partner[ch]][0]
         n_off = len(_bits(topo.mask(far_w, core)))
@@ -171,31 +220,24 @@ def rank_program(g, core, T, topo):
         started = set()
 
         def mm(qq, rhs, stop=False):
-            ins = pe.matmul(T["ps%d" % qq][:, 0:Q], T.hs[:, :], rhs, qq not in started, stop)
+            ins2 = pe.matmul(T["ps%d" % qq][:, 0:Q], T.hs[:, :], rhs, qq not in started, stop)
             started.add(qq)
-            return ins
+            return ins2
 
         pe.wait_ge(sem.ldh, 16)
-        if myq is not None:
-            pe.wait_ge(sem.gv, nv)
-            pe.wait_ge(sem.gs, W - nv)
-            mm(myq, piece(T.S, myq))
-            pe.wait_ge(sem.s1, E1 * (len(sk) - 1))
-            for i, s in enumerate(sk):
-                if s != core:
-                    mm(myq, T["p%d" % i][:, :])
         rem = [qq for qq in range(W) if qq != myq]
         pe.wait_ge(sem.xc, n_on * len(rem))
         for qq in rem:
             mm(qq, piece(T.xc, qq))
         if myq is not None:
-            pe.wait_ge(sem.s2, n_off * 3)
-            for b in (T.r0, T.r1, T.r2):
-                mm(myq, b[:, :])
+            pe.wait_ge(sem.vx, GS - 2)
+            mm(myq, T["b%d" % (GS - 3)][:, :])
+            pe.wait_ge(sem["s2%d" % frm[-1]], n_off)
+            mm(myq, last[:, :])
+        for qq in rem:
+            pe.wait_ge(sem["xr%d" % qq], n_on)
+            mm(qq, piece(T.xr, qq))
         for qq in range(W):
-            if qq != myq:
-                pe.wait_ge(sem["xr%d" % qq], n_on)
-                mm(qq, piece(T.xr, qq))
             pe.wait_ge(sem["xo%d" % qq], n_off)
             mm(qq, piece(T.xo, qq), True).then_inc(sem["mm%d" % qq], 1)
         for qq in range(W):
@@ -204,7 +246,7 @@ def rank_program(g, core, T, topo):
                 v.tensor_copy(piece(T.ysb, qq), T["ps%d" % qq][:, 0:Q]).then_inc(sem.cpv, 1)
             else:
                 sc.wait_ge(sem["mm%d" % qq], 1)
-                sc.activation(piece(T.ysb, qq), T["ps%d" % qq][:, 0:Q], ActivationFunctionType.Copy).then_inc(sem.cps, 1)
+                sc.activation(piece(T.ysb, qq), T["ps%d" % qq][:, 0:Q], COPY).then_inc(sem.cps, 1)
         sy.wait_ge(sem.cpv, nv)
         sy.dma_start(T.y[:, 0:nv * Q], T.ysb[:, 0:nv * Q]).then_inc(sem.st, 16)
         sc.wait_ge(sem.cps, W - nv)

@@ -13,9 +13,12 @@ E1 = 16 // W
 SCRATCH = {
     "negs": ("sbuf", [128, NS // 16], "int32"),
     "offs": ("sbuf", [128, NS // 16], "uint16"),
+    "offs2": ("sbuf", [128, NS // 16], "uint16"),
     "win": ("sbuf", [128, WIN], "bfloat16"),
+    "win2": ("sbuf", [128, WIN], "bfloat16"),
     "hs": ("sbuf", [128, TOK], "bfloat16"),
     "S": ("sbuf", [128, NS], "bfloat16"),
+    "S2": ("sbuf", [128, NS], "bfloat16"),
     "p0": ("sbuf", [128, Q], "bfloat16"),
     "p1": ("sbuf", [128, Q], "bfloat16"),
     "am": ("sbuf", [128, Q], "bfloat16"),
@@ -35,10 +38,10 @@ for _q in range(W):
 for _q in range(GS):
     SCRATCH["r%d" % _q] = ("sbuf", [128, Q], "bfloat16")
 
-SEMAPHORES = ["ldn", "ldt", "ldh", "ms", "so", "gv", "gs", "gv2", "gs2", "s1", "xc", "ls", "cpv", "cps", "st",
+SEMAPHORES = ["ldn", "ldt", "ldh", "ms", "so", "so2", "gv", "gs", "gv2", "gs2", "g2v", "g2s", "tb", "s1", "xc", "ls", "st",
               "va", "vx", "mi", "idn", "pr", "sr"]
 SEMAPHORES += ["xr%d" % _q for _q in range(W)] + ["xo%d" % _q for _q in range(W)] + ["mm%d" % _q for _q in range(W)]
-SEMAPHORES += ["s2%d" % _q for _q in range(GS)]
+SEMAPHORES += ["s2%d" % _q for _q in range(GS)] + ["cp%d" % _q for _q in range(W)]
 
 
 def _bits(mask):
@@ -112,60 +115,78 @@ def rank_program(g, core, T, topo):
         for k in range(8):
             (sy if k < 3 else sc).dma_start(T.negs[16 * k:16 * k + 16, :], T.neg[:, :]).then_inc(sem.ldn, 16)
         sy.dma_start(T.hs[:, :], T.h[:, :]).then_inc(sem.ldh, 16)
-        v.memset(T.win[:, 0:PAD], 0.0).then_inc(sem.ms, 1)
-        v.memset(T.win[:, PAD + R:WIN], 0.0).then_inc(sem.ms, 1)
+        for wn in (T.win, T.win2):
+            v.memset(wn[:, 0:PAD], 0.0).then_inc(sem.ms, 1)
+            v.memset(wn[:, PAD + R:WIN], 0.0).then_inc(sem.ms, 1)
     if is_worker:
         v.memset(T.ones[:, :], 1.0).then_inc(sem.mi, 1)
         g.wait_ge(sem.mi, 1)
         g.affine_select(T.ident[:, :], T.ones[:, :], [[-1, 128]], AluOpType.is_equal, 0.0, 0, 1).then_inc(sem.idn, 1)
     if rank is not None:
+        other = [s for s in sk if s != core][0]
+        helpers = [(q, w) for q, w in enumerate(workers[ch]) if w not in sk]
+        eb = _bits(topo.mask(core, other))
+        te = eb[E1 * len(helpers):E1 * len(helpers) + E1]
+        g.wait_ge(sem.ldt, 16)
+        g.remote_dma_fused([RemoteDMATransfer(dst_ids=[_dst(topo, other)], dma_engine_mask=_mk(te), remote_sem=sem.tb,
+                                              src=T.win[:, PAD:PAD + R], dst=T.win2[:, PAD:PAD + R])], local_sem=sem.ls)
+        sent[0] += len(te)
         v.wait_ge(sem.ldn, 128)
         v.tensor_scalar(T.offs[:, :], T.negs[:, :], PAD - R * rank, PAD + R, ADD, AluOpType.min).then_inc(sem.so, 1)
         for eng in (v, sc):
             eng.wait_ge(sem.so, 1)
-            eng.wait_ge(sem.ms, 2)
+            eng.wait_ge(sem.ms, 4)
             eng.wait_ge(sem.ldt, 16)
 
-        def gath(a, b):
-            return T.S[:, a:b], T.win[:, 0:WIN].indirect(T.offs[:, a // 16:b // 16])
+        def gath(dst, wn, of, a, b):
+            return dst[:, a:b], wn[:, 0:WIN].indirect(of[:, a // 16:b // 16])
 
         late = Q * len([w for w in workers[ch] if w in sk])
         mid = late + (NS - late) // 2
-        o, i_ = gath(late, mid)
+        o, i_ = gath(T.S, T.win, T.offs, late, mid)
         v.tensor_copy(o, i_).then_inc(sem.gv, 1)
-        o, i_ = gath(mid, NS)
+        o, i_ = gath(T.S, T.win, T.offs, mid, NS)
         sc.activation(o, i_, COPY).then_inc(sem.gs, 1)
-        o, i_ = gath(0, late // 2)
+        o, i_ = gath(T.S, T.win, T.offs, 0, late // 2)
         v.tensor_copy(o, i_).then_inc(sem.gv2, 1)
-        o, i_ = gath(late // 2, late)
+        o, i_ = gath(T.S, T.win, T.offs, late // 2, late)
         sc.activation(o, i_, COPY).then_inc(sem.gs2, 1)
+        g.wait_ge(sem.gv, 1)
+        g.wait_ge(sem.gs, 1)
         slot = "p%d" % sk.index(core)
-        others = [(q, w) for q, w in enumerate(workers[ch]) if w != core]
-        eb = _bits(topo.mask(core, others[0][1]))
-        calls = [[(q, w) for q, w in others if w not in sk], [(q, w) for q, w in others if w in sk]]
-        used = 0
-        for n, lst in enumerate(calls):
-            g.wait_ge(sem.gv2 if n else sem.gv, 1)
-            g.wait_ge(sem.gs2 if n else sem.gs, 1)
-            tr = []
-            for q, w in lst:
-                tr.append(RemoteDMATransfer(dst_ids=[_dst(topo, w)], dma_engine_mask=_mk(eb[used:used + E1]),
-                                            remote_sem=sem.s1, src=piece(T.S, q), dst=T[slot][:, :]))
-                used += E1
-                sent[0] += E1
-            if tr:
-                g.remote_dma_fused(tr, local_sem=sem.ls)
+        tr = []
+        for i, (q, w) in enumerate(helpers):
+            tr.append(RemoteDMATransfer(dst_ids=[_dst(topo, w)], dma_engine_mask=_mk(eb[i * E1:(i + 1) * E1]),
+                                        remote_sem=sem.s1, src=piece(T.S, q), dst=T[slot][:, :]))
+            sent[0] += E1
+        g.remote_dma_fused(tr, local_sem=sem.ls)
+        v.tensor_scalar(T.offs2[:, :], T.negs[:, :], PAD - R * T.rank_of(other), PAD + R, ADD, AluOpType.min).then_inc(sem.so2, 1)
+        a2, b2 = (myq * Q, (myq + 1) * Q) if is_worker else (0, NS)
+        m2 = (a2 + b2) // 2
+        for eng in (v, sc):
+            eng.wait_ge(sem.so2, 1)
+            eng.wait_ge(sem.tb, len(te))
+        o, i_ = gath(T.S2, T.win2, T.offs2, a2, m2)
+        v.tensor_copy(o, i_).then_inc(sem.g2v, 1)
+        o, i_ = gath(T.S2, T.win2, T.offs2, m2, b2)
+        sc.activation(o, i_, COPY).then_inc(sem.g2s, 1)
 
     if is_worker:
         q = myq
-        mine = [piece(T.S, q) if s == core else T["p%d" % i][:, :] for i, s in enumerate(sk)]
+        if rank is None:
+            mine = [T.p0[:, :], T.p1[:, :]]
+            ready = [(sem.s1, E1 * len(sk))]
+        else:
+            mine = [piece(T.S, q), piece(T.S2, q)]
+            ready = [(sem.gv2, 1), (sem.gs2, 1), (sem.g2v, 1), (sem.g2s, 1)]
         gr = group[ch]
         gi = gr.index(ch)
         to = [gr[(gi + k) % GS] for k in range(1, GS)]
         frm = [(gi - k) % GS for k in range(1, GS)]
         last = T["r%d" % frm[-1]]
-        far = sinks[partner[ch]]
-        near = [s for s in sk if s != core]
+        turn = 1 if q < nv else -1
+        far = sinks[partner[ch]][::turn]
+        near = [s for s in sk[::turn] if s != core]
         off = topo.mask(core, far[0])
         for c2 in to:
             off &= topo.mask(core, workers[c2][q])
@@ -173,19 +194,20 @@ def rank_program(g, core, T, topo):
             off &= topo.mask(core, s)
         on = topo.mask(core, near[0]) & ~off
         noff, non = len(_bits(off)), len(_bits(on))
-        g.wait_ge(sem.s1, E1 * len(near))
+        for s_, n_ in ready:
+            g.wait_ge(s_, n_)
         g.remote_dma_fused([RemoteDMATransfer(dst_ids=[_dst(topo, workers[c2][q]) for c2 in to], dma_engine_mask=off,
                                               remote_sem=sem["s2%d" % gi], srcs=mine,
                                               dsts=[T["r%d" % gi][:, :] for c2 in to], alu_op=1)], local_sem=sem.ls)
         sent[0] += noff
-        g.remote_dma_fused([RemoteDMATransfer(dst_ids=[_dst(topo, s) for s in near], dma_engine_mask=on,
-                                              remote_sem=sem.xc, srcs=mine,
-                                              dsts=[piece(T.xc, q) for s in near], alu_op=1)], local_sem=sem.ls)
-        sent[0] += non
-        v.wait_ge(sem.s1, E1 * len(near))
-        if rank is not None:
-            v.wait_ge(sem.gv2, 1)
-            v.wait_ge(sem.gs2, 1)
+        wants = [s for s in near if s in workers[ch]]
+        if wants:
+            g.remote_dma_fused([RemoteDMATransfer(dst_ids=[_dst(topo, s) for s in wants], dma_engine_mask=on,
+                                                  remote_sem=sem.xc, srcs=mine,
+                                                  dsts=[piece(T.xc, q) for s in wants], alu_op=1)], local_sem=sem.ls)
+            sent[0] += non
+        for s_, n_ in ready:
+            v.wait_ge(s_, n_)
         v.tensor_tensor(T.am[:, :], mine[0], mine[1], ADD).then_inc(sem.va, 1)
         v.wait_ge(sem.va, 1)
         pe.wait_ge(sem.idn, 1)
@@ -224,32 +246,46 @@ def rank_program(g, core, T, topo):
             started.add(qq)
             return ins2
 
+        lo, hi = list(range(nv)), list(range(nv, W))
+        halves = [lo, hi] if sk.index(core) == 0 else [hi, lo]
         pe.wait_ge(sem.ldh, 16)
         rem = [qq for qq in range(W) if qq != myq]
-        pe.wait_ge(sem.xc, n_on * len(rem))
-        for qq in rem:
-            mm(qq, piece(T.xc, qq))
-        if myq is not None:
+        if myq is None:
+            for s_ in (sem.gv, sem.gs, sem.gv2, sem.gs2):
+                pe.wait_ge(s_, 1)
+            for qq in rem:
+                mm(qq, piece(T.S, qq))
+            pe.wait_ge(sem.g2v, 1)
+            pe.wait_ge(sem.g2s, 1)
+            for qq in rem:
+                mm(qq, piece(T.S2, qq))
+        else:
+            pe.wait_ge(sem.xc, n_on * len(rem))
+            for qq in rem:
+                mm(qq, piece(T.xc, qq))
             pe.wait_ge(sem.vx, GS - 2)
             mm(myq, T["b%d" % (GS - 3)][:, :])
             pe.wait_ge(sem["s2%d" % frm[-1]], n_off)
             mm(myq, last[:, :])
-        for qq in rem:
-            pe.wait_ge(sem["xr%d" % qq], n_on)
-            mm(qq, piece(T.xr, qq))
-        for qq in range(W):
-            pe.wait_ge(sem["xo%d" % qq], n_off)
-            mm(qq, piece(T.xo, qq), True).then_inc(sem["mm%d" % qq], 1)
-        for qq in range(W):
-            if qq < nv:
-                v.wait_ge(sem["mm%d" % qq], 1)
-                v.tensor_copy(piece(T.ysb, qq), T["ps%d" % qq][:, 0:Q]).then_inc(sem.cpv, 1)
-            else:
-                sc.wait_ge(sem["mm%d" % qq], 1)
-                sc.activation(piece(T.ysb, qq), T["ps%d" % qq][:, 0:Q], COPY).then_inc(sem.cps, 1)
-        sy.wait_ge(sem.cpv, nv)
-        sy.dma_start(T.y[:, 0:nv * Q], T.ysb[:, 0:nv * Q]).then_inc(sem.st, 16)
-        sc.wait_ge(sem.cps, W - nv)
-        sc.dma_start(T.y[:, nv * Q:NS], T.ysb[:, nv * Q:NS]).then_inc(sem.st, 16)
+        for n, hf in enumerate(halves):
+            for qq in hf:
+                if qq != myq:
+                    pe.wait_ge(sem["xr%d" % qq], n_on)
+                    mm(qq, piece(T.xr, qq))
+            for qq in hf:
+                pe.wait_ge(sem["xo%d" % qq], n_off)
+                mm(qq, piece(T.xo, qq), True).then_inc(sem["mm%d" % qq], 1)
+            for j, qq in enumerate(hf):
+                if j % 2 == 0:
+                    v.wait_ge(sem["mm%d" % qq], 1)
+                    v.tensor_copy(piece(T.ysb, qq), T["ps%d" % qq][:, 0:Q]).then_inc(sem["cp%d" % qq], 1)
+                else:
+                    sc.wait_ge(sem["mm%d" % qq], 1)
+                    sc.activation(piece(T.ysb, qq), T["ps%d" % qq][:, 0:Q], COPY).then_inc(sem["cp%d" % qq], 1)
+            dq = sc if n else sy
+            for qq in hf:
+                dq.wait_ge(sem["cp%d" % qq], 1)
+            a, b = hf[0] * Q, (hf[-1] + 1) * Q
+            dq.dma_start(T.y[:, a:b], T.ysb[:, a:b]).then_inc(sem.st, 16)
         g.wait_ge(sem.st, 32)
     g.wait_ge(sem.ls, sent[0])

from concourse.bass import DstId, RemoteDMATransfer
from concourse.mybir import AluOpType, ActivationFunctionType

N, R, NS, TOK = 16, 256, 512, 128
WPD = 2
W = 4
Q = NS // W
GS = 4
PAD = 8
WIN = R + 2 * PAD
E1 = 16 // W

SCRATCH = {
    "negs": ("sbuf", [128, NS // 16], "int32"),
    "offs": ("sbuf", [128, NS // 16], "uint16"),
    "offs2": ("sbuf", [128, NS // 16], "uint16"),
    "win": ("sbuf", [128, WIN], "bfloat16"),
    "win2": ("sbuf", [128, WIN], "bfloat16"),
    "hs": ("sbuf", [128, TOK], "bfloat16"),
    "S": ("sbuf", [128, NS], "bfloat16"),
    "S2": ("sbuf", [128, NS], "bfloat16"),
    "p0": ("sbuf", [128, Q], "bfloat16"),
    "p1": ("sbuf", [128, Q], "bfloat16"),
    "am": ("sbuf", [128, Q], "bfloat16"),
    "b0": ("sbuf", [128, Q], "bfloat16"),
    "b1": ("sbuf", [128, Q], "bfloat16"),
    "xrs": ("sbuf", [128, Q], "bfloat16"),
    "ones": ("sbuf", [128, 128], "bfloat16"),
    "ident": ("sbuf", [128, 128], "bfloat16"),
    "xc": ("sbuf", [128, NS], "bfloat16"),
    "xr": ("sbuf", [128, NS], "bfloat16"),
    "xo": ("sbuf", [128, NS], "bfloat16"),
    "ysb": ("sbuf", [128, NS], "bfloat16"),
    "psr": ("psum", [128, 512], "float32"),
}
for _q in range(W):
    SCRATCH["ps%d" % _q] = ("psum", [128, 512], "float32")
for _q in range(GS):
    SCRATCH["r%d" % _q] = ("sbuf", [128, Q], "bfloat16")

SEMAPHORES = ["ldn", "ldt", "ldh", "ms", "so", "so2", "gv", "gs", "gv2", "gs2", "g2v", "g2s", "tb", "s1", "xc", "ls", "st",
              "va", "vx", "mi", "idn", "pr", "sr"]
SEMAPHORES += ["xr%d" % _q for _q in range(W)] + ["xo%d" % _q for _q in range(W)] + ["mm%d" % _q for _q in range(W)]
SEMAPHORES += ["s2%d" % _q for _q in range(GS)] + ["cp%d" % _q for _q in range(W)]


def _bits(mask):
    return [b for b in range(mask.bit_length()) if (mask >> b) & 1]


def _mk(bits):
    return sum(1 << b for b in bits)


def _plan(T, topo):
    ranks = list(T.cores)
    ncore = topo.CHIPS * topo.CORES_PER_CHIP
    chips = sorted(set(topo.chip(c) for c in ranks))
    sinks = {ch: [c for c in ranks if topo.chip(c) == ch] for ch in chips}
    workers = {}
    for ch in chips:
        able = [k for k in range(ncore) if topo.chip(k) == ch and all(topo.may_write(k, d) for d in ranks if d != k)]
        able.sort(key=lambda k: (0 if k in ranks else 1, k))
        pick = []
        for dd in sorted(set(topo.die(k) for k in able)):
            pick += [k for k in able if topo.die(k) == dd][:WPD]
        pick.sort(key=lambda k: (0 if k in ranks else 1, topo.die(k), k))
        workers[ch] = pick
    first = [ch for ch in chips if ch == chips[0] or topo.same_plane(ch, chips[0])]
    order = first + [ch for ch in chips if ch not in first]
    groups = [order[:GS], order[GS:]]
    partner, free = {}, list(groups[1])
    for a in groups[0]:
        m = [b for b in free if topo.mates(a, b)]
        if m:
            partner[a] = m[0]
            free.remove(m[0])
    for a in groups[0]:
        if a not in partner:
            partner[a] = free.pop(0)
    for a, b in list(partner.items()):
        partner[b] = a
    group = {ch: gr for gr in groups for ch in gr}
    return sinks, workers, group, partner


def _dst(topo, c):
    rid, pid, _se = topo.addr(c)
    return DstId(rid=rid, pnc=pid)


def rank_program(g, core, T, topo):
    sinks, workers, group, partner = _plan(T, topo)
    ch = topo.chip(core)
    if ch not in sinks:
        return
    rank = T.rank_of(core)
    is_worker = core in workers[ch]
    if rank is None and not is_worker:
        return
    sem = T.sem
    sk = sinks[ch]
    sent = [0]
    nv = W // 2
    myq = workers[ch].index(core) if is_worker else None
    sy, sc, v, pe = g.sync, g.scalar, g.vector, g.tensor
    ADD = AluOpType.add
    COPY = ActivationFunctionType.Copy

    def piece(buf, q):
        return buf[:, q * Q:(q + 1) * Q]

    if rank is not None:
        sy.dma_start(T.win[:, PAD:PAD + R], T.tab[:, :]).then_inc(sem.ldt, 16)
        for k in range(8):
            (sy if k < 3 else sc).dma_start(T.negs[16 * k:16 * k + 16, :], T.neg[:, :]).then_inc(sem.ldn, 16)
        sy.dma_start(T.hs[:, :], T.h[:, :]).then_inc(sem.ldh, 16)
        for wn in (T.win, T.win2):
            v.memset(wn[:, 0:PAD], 0.0).then_inc(sem.ms, 1)
            v.memset(wn[:, PAD + R:WIN], 0.0).then_inc(sem.ms, 1)
    if is_worker:
        v.memset(T.ones[:, :], 1.0).then_inc(sem.mi, 1)
        g.wait_ge(sem.mi, 1)
        g.affine_select(T.ident[:, :], T.ones[:, :], [[-1, 128]], AluOpType.is_equal, 0.0, 0, 1).then_inc(sem.idn, 1)
    if rank is not None:
        other = [s for s in sk if s != core][0]
        helpers = [(q, w) for q, w in enumerate(workers[ch]) if w not in sk]
        eb = _bits(topo.mask(core, other))
        te = eb[E1 * len(helpers):E1 * len(helpers) + E1]
        g.wait_ge(sem.ldt, 16)
        g.remote_dma_fused([RemoteDMATransfer(dst_ids=[_dst(topo, other)], dma_engine_mask=_mk(te), remote_sem=sem.tb,
                                              src=T.win[:, PAD:PAD + R], dst=T.win2[:, PAD:PAD + R])], local_sem=sem.ls)
        sent[0] += len(te)
        v.wait_ge(sem.ldn, 128)
        v.tensor_scalar(T.offs[:, :], T.negs[:, :], PAD - R * rank, PAD + R, ADD, AluOpType.min).then_inc(sem.so, 1)
        for eng in (v, sc):
            eng.wait_ge(sem.so, 1)
            eng.wait_ge(sem.ms, 4)
            eng.wait_ge(sem.ldt, 16)

        def gath(dst, wn, of, a, b):
            return dst[:, a:b], wn[:, 0:WIN].indirect(of[:, a // 16:b // 16])

        late = Q * len([w for w in workers[ch] if w in sk])
        mid = late + (NS - late) // 2
        o, i_ = gath(T.S, T.win, T.offs, late, mid)
        v.tensor_copy(o, i_).then_inc(sem.gv, 1)
        o, i_ = gath(T.S, T.win, T.offs, mid, NS)
        sc.activation(o, i_, COPY).then_inc(sem.gs, 1)
        o, i_ = gath(T.S, T.win, T.offs, 0, late // 2)
        v.tensor_copy(o, i_).then_inc(sem.gv2, 1)
        o, i_ = gath(T.S, T.win, T.offs, late // 2, late)
        sc.activation(o, i_, COPY).then_inc(sem.gs2, 1)
        g.wait_ge(sem.gv, 1)
        g.wait_ge(sem.gs, 1)
        slot = "p%d" % sk.index(core)
        tr = []
        for i, (q, w) in enumerate(helpers):
            tr.append(RemoteDMATransfer(dst_ids=[_dst(topo, w)], dma_engine_mask=_mk(eb[i * E1:(i + 1) * E1]),
                                        remote_sem=sem.s1, src=piece(T.S, q), dst=T[slot][:, :]))
            sent[0] += E1
        g.remote_dma_fused(tr, local_sem=sem.ls)
        v.tensor_scalar(T.offs2[:, :], T.negs[:, :], PAD - R * T.rank_of(other), PAD + R, ADD, AluOpType.min).then_inc(sem.so2, 1)
        a2, b2 = (myq * Q, (myq + 1) * Q) if is_worker else (0, NS)
        m2 = (a2 + b2) // 2
        for eng in (v, sc):
            eng.wait_ge(sem.so2, 1)
            eng.wait_ge(sem.tb, len(te))
        o, i_ = gath(T.S2, T.win2, T.offs2, a2, m2)
        v.tensor_copy(o, i_).then_inc(sem.g2v, 1)
        o, i_ = gath(T.S2, T.win2, T.offs2, m2, b2)
        sc.activation(o, i_, COPY).then_inc(sem.g2s, 1)

    if is_worker:
        q = myq
        if rank is None:
            mine = [T.p0[:, :], T.p1[:, :]]
            ready = [(sem.s1, E1 * len(sk))]
        else:
            mine = [piece(T.S, q), piece(T.S2, q)]
            ready = [(sem.gv2, 1), (sem.gs2, 1), (sem.g2v, 1), (sem.g2s, 1)]
        gr = group[ch]
        gi = gr.index(ch)
        to = [gr[(gi + k) % GS] for k in range(1, GS)]
        frm = [(gi - k) % GS for k in range(1, GS)]
        last = T["r%d" % frm[-1]]
        turn = 1 if q < nv else -1
        far = sinks[partner[ch]][::turn]
        near = [s for s in sk[::turn] if s != core]
        off = topo.mask(core, far[0])
        for c2 in to:
            off &= topo.mask(core, workers[c2][q])
        for s in far:
            off &= topo.mask(core, s)
        on = topo.mask(core, near[0]) & ~off
        noff, non = len(_bits(off)), len(_bits(on))
        for s_, n_ in ready:
            g.wait_ge(s_, n_)
        g.remote_dma_fused([RemoteDMATransfer(dst_ids=[_dst(topo, workers[c2][q]) for c2 in to], dma_engine_mask=off,
                                              remote_sem=sem["s2%d" % gi], srcs=mine,
                                              dsts=[T["r%d" % gi][:, :] for c2 in to], alu_op=1)], local_sem=sem.ls)
        sent[0] += noff
        wants = [s for s in near if s in workers[ch]]
        if wants:
            g.remote_dma_fused([RemoteDMATransfer(dst_ids=[_dst(topo, s) for s in wants], dma_engine_mask=on,
                                                  remote_sem=sem.xc, srcs=mine,
                                                  dsts=[piece(T.xc, q) for s in wants], alu_op=1)], local_sem=sem.ls)
            sent[0] += non
        for s_, n_ in ready:
            v.wait_ge(s_, n_)
        v.tensor_tensor(T.am[:, :], mine[0], mine[1], ADD).then_inc(sem.va, 1)
        v.wait_ge(sem.va, 1)
        pe.wait_ge(sem.idn, 1)
        prev = T.am
        for k, s in enumerate(frm[:-1]):
            arr = T["r%d" % s]
            v.wait_ge(sem["s2%d" % s], noff)
            v.wait_ge(sem.vx, k)
            v.tensor_tensor(T["b%d" % k][:, :], prev[:, :], arr[:, :], ADD).then_inc(sem.vx, 1)
            prev = T["b%d" % k]
            pe.wait_ge(sem["s2%d" % s], noff)
            ins = pe.matmul(T.psr[:, 0:Q], T.ident[:, :], arr[:, :], k == 0, k == GS - 3)
        ins.then_inc(sem.pr, 1)
        sc.wait_ge(sem.pr, 1)
        sc.activation(T.xrs[:, :], T.psr[:, 0:Q], COPY).then_inc(sem.sr, 1)
        g.wait_ge(sem.vx, GS - 2)
        g.wait_ge(sem.sr, 1)
        g.wait_ge(sem["s2%d" % frm[-1]], noff)
        g.remote_dma_fused([
            RemoteDMATransfer(dst_ids=[_dst(topo, s) for s in far], dma_engine_mask=off, remote_sem=sem["xo%d" % q],
                              srcs=[prev[:, :], last[:, :]], dsts=[piece(T.xo, q) for s in far], alu_op=1),
            RemoteDMATransfer(dst_ids=[_dst(topo, s) for s in near], dma_engine_mask=on, remote_sem=sem["xr%d" % q],
                              srcs=[T.xrs[:, :], last[:, :]], dsts=[piece(T.xr, q) for s in near], alu_op=1),
        ], local_sem=sem.ls)
        sent[0] += noff + non

    if rank is not None:
        some = [w for w in workers[ch] if w != core][0]
        far_w = workers[partner[ch]][0]
        n_off = len(_bits(topo.mask(far_w, core)))
        n_on = len(_bits(topo.mask(some, core) & ~topo.mask(some, sinks[partner[ch]][0])))
        started = set()

        def mm(qq, rhs, stop=False):
            ins2 = pe.matmul(T["ps%d" % qq][:, 0:Q], T.hs[:, :], rhs, qq not in started, stop)
            started.add(qq)
            return ins2

        lo, hi = list(range(nv)), list(range(nv, W))
        halves = [lo, hi] if sk.index(core) == 0 else [hi, lo]
        pe.wait_ge(sem.ldh, 16)
        rem = [qq for qq in range(W) if qq != myq]
        if myq is None:
            for s_ in (sem.gv, sem.gs, sem.gv2, sem.gs2):
                pe.wait_ge(s_, 1)
            for qq in rem:
                mm(qq, piece(T.S, qq))
            pe.wait_ge(sem.g2v, 1)
            pe.wait_ge(sem.g2s, 1)
            for qq in rem:
                mm(qq, piece(T.S2, qq))
        else:
            pe.wait_ge(sem.xc, n_on * len(rem))
            for qq in rem:
                mm(qq, piece(T.xc, qq))
            pe.wait_ge(sem.vx, GS - 2)
            mm(myq, T["b%d" % (GS - 3)][:, :])
            pe.wait_ge(sem["s2%d" % frm[-1]], n_off)
            mm(myq, last[:, :])
        for n, hf in enumerate(halves):
            for qq in hf:
                if qq != myq:
                    pe.wait_ge(sem["xr%d" % qq], n_on)
                    mm(qq, piece(T.xr, qq))
            for qq in hf:
                pe.wait_ge(sem["xo%d" % qq], n_off)
                mm(qq, piece(T.xo, qq), True).then_inc(sem["mm%d" % qq], 1)
            for j, qq in enumerate(hf):
                if j % 2 == 0:
                    v.wait_ge(sem["mm%d" % qq], 1)
                    v.tensor_copy(piece(T.ysb, qq), T["ps%d" % qq][:, 0:Q]).then_inc(sem["cp%d" % qq], 1)
                else:
                    sc.wait_ge(sem["mm%d" % qq], 1)
                    sc.activation(piece(T.ysb, qq), T["ps%d" % qq][:, 0:Q], COPY).then_inc(sem["cp%d" % qq], 1)
            dq = sc if n else sy
            for qq in hf:
                dq.wait_ge(sem["cp%d" % qq], 1)
            a, b = hf[0] * Q, (hf[-1] + 1) * Q
            dq.dma_start(T.y[:, a:b], T.ysb[:, a:b]).then_inc(sem.st, 16)
        g.wait_ge(sem.st, 32)
    g.wait_ge(sem.ls, sent[0])
